import numpy as np
import ml_dtypes


def mxq(x, axis, fmt="e4m3"):
    dtype, down = {"e4m3": (ml_dtypes.float8_e4m3fn, 7), "e5m2": (ml_dtypes.float8_e5m2, 14)}[fmt]
    v = np.moveaxis(np.asarray(x, np.float32).astype(ml_dtypes.bfloat16).astype(np.float64), axis, -1)
    blocks = v.reshape(v.shape[:-1] + (-1, 32))
    amax = np.abs(blocks).max(-1, keepdims=True)
    byte = np.maximum(np.where(amax > 0, np.frexp(amax)[1] - 1 + 127, 0) - down, 1)
    scale = np.exp2(byte - 127.0)
    codes = (blocks / scale).astype(np.float32).astype(dtype).astype(np.float64)
    return np.moveaxis((codes * scale).reshape(v.shape), -1, axis)


WIDE = False


def mx_kscale(k):
    if not WIDE:
        return np.ones(k)
    levels = np.array([10, -10, 5, -5, 0])
    if k % 512:
        return np.exp2(np.random.permutation(np.resize(levels, k // 32))).repeat(32)
    a = np.empty((k // 512, 16))
    for p in range(k // 512):
        a[p, :8] = np.random.permutation(np.resize(levels, 8))
        for g in range(8):
            far = levels[np.abs(levels - a[p, g]) >= 10]
            a[p, g + 8] = far[np.random.randint(len(far))]
    return np.exp2(a.ravel()).repeat(32)


def f64(x):
    return np.asarray(x).astype(np.float64)


def striped(idx):
    return np.tile(idx.reshape(-1, 16).T, (8, 1)).astype(np.uint16)


def unstriped(offs):
    return offs[:16].T.reshape(-1).astype(np.int64)


def pack_weight(w):
    k, n = w.shape
    w = f64(np.asarray(w, np.float32).astype(ml_dtypes.bfloat16)).reshape(k // 32, 32, n)
    amax = np.abs(w).max(1)
    byte = np.clip(np.where(amax > 0, np.frexp(amax)[1] - 1 + 127 - 7, 1), 1, 254)
    scaled = (w * np.exp2(127.0 - byte)[:, None, :]).reshape(k, n).astype(np.float32)
    words = np.ascontiguousarray(scaled.reshape(k // 512, 128, 4, n).transpose(0, 1, 3, 2)).astype(ml_dtypes.float8_e4m3fn).view(np.uint8)
    return words, np.ascontiguousarray(byte.astype(np.uint8).reshape(k // 512, 16, n))


def unpack_weight(words, scales):
    g, p, n, _ = words.shape
    vals = np.ascontiguousarray(words).view(ml_dtypes.float8_e4m3fn).astype(np.float64) * np.repeat(np.exp2(scales.astype(np.float64) - 127.0), 8, axis=1)[..., None]
    return vals.transpose(0, 1, 3, 2).reshape(g * 512, n)


K, T, S, N, H, U, W = 512, 2048, 512, 256, 512, 1024, 1024


def setup_inputs():
    n = np.random.standard_normal
    s = mx_kscale(K)[:, None]
    u = mx_kscale(H)
    packed_xT = pack_weight(n((K, T)) * s)
    packed_eT = pack_weight(n((K, W)) * s)
    return {
        "x_words": packed_xT[0],
        "x_scales": packed_xT[1],
        "w1": (n((K, H)) / np.sqrt(K) / s).astype(np.float32),
        "e_words": packed_eT[0],
        "e_scales": packed_eT[1],
        "w2": (n((K, H)) / np.sqrt(K) / s).astype(np.float32),
        "gn": (np.random.uniform(0.4, 1.6, (H, U))).astype(np.float32),
        "unit": (np.random.uniform(0.6, 1.4, (H, 1)) * u[:, None]).astype(np.float32),
        "w3": (n((H, N)) / np.sqrt(H) / u[:, None]).astype(np.float32),
        "feat": (n((N, U))).astype(np.float32),
        "offs": striped(np.random.permutation(T)[:S]),
        "lv2": striped(np.random.permutation(W)[:S]),
        "c1": striped(np.random.permutation(np.concatenate([np.arange(S), np.random.randint(0, S, U - S)]))),
        "c2": striped(np.random.permutation(np.concatenate([np.arange(S), np.random.randint(0, S, U - S)]))),
    }


def reference(x_words, x_scales, w1, e_words, e_scales, w2, gn, unit, w3, feat, offs, lv2, c1, c2):
    xq = unpack_weight(x_words, x_scales)[:, unstriped(offs)]
    y = mxq(f64(w1), 0, "e4m3").T @ xq
    s1 = y[:, unstriped(c1)]
    e_lv2 = unpack_weight(e_words, e_scales)[:, unstriped(lv2)]
    ye = mxq(f64(w2), 0, "e4m3").T @ e_lv2
    s2 = ye[:, unstriped(c2)]
    rec = s1 + f64(gn) * s2
    act = np.maximum(rec, 0.7 * y[:, unstriped(c2)])
    hid = f64(unit) * act
    rr = mxq(f64(w3), 0, "e4m3").T @ mxq(hid, 0, "e4m3")
    return rr * f64(feat)

@@ -1,0 +1,245 @@
+from contextlib import ExitStack
+
+import concourse.mybir as mybir
+
+K, T, S, N, H, U, W = 512, 2048, 512, 256, 512, 1024, 1024
+FLOPS = 2 * (2 * K * H * S + H * N * U)
+
+F32 = mybir.dt.float32
+BF16 = mybir.dt.bfloat16
+I32 = mybir.dt.int32
+U32 = mybir.dt.uint32
+U16 = mybir.dt.uint16
+U8 = mybir.dt.uint8
+FP8X4 = mybir.dt.float8_e4m3fn_x4
+ALU = mybir.AluOpType
+COPY = mybir.ActivationFunctionType.Copy
+
+P = 128
+PACK = 4
+LIST = 16
+SPARE = 16
+HALF = 512
+CHUNKS = ((0, 512), (512, 256), (768, 256))
+
+
+def tile_picked_ysemid_max_p_kernel(
+    tc, x_words, x_scales, w1, e_words, e_scales, w2, gn, unit, w3, feat, offs, lv2, c1, c2, out
+):
+    nc = tc.nc
+    with ExitStack() as ctx:
+        keep = ctx.enter_context(tc.tile_pool(name="keep", bufs=1))
+        psum = ctx.enter_context(tc.psum_pool(name="psum", bufs=8))
+
+        def sbuf(name, shape, dtype):
+            return keep.tile(shape, dtype, name=name, align_bytes=64)
+
+        def load_list(name, src):
+            tile = keep.tile(list(src.shape), U16, name=name)
+            nc.sync.dma_start(tile[:], src)
+            return tile
+
+        def load_words(name, words, queue):
+            tile = sbuf(name, [P, words.shape[2]], U32)
+            queue.dma_start(tile[:].bitcast(I32), words[0].rearrange("p n t -> p (n t)").bitcast(I32))
+            return tile
+
+        def load_scales(name, scales, queue):
+            tile = sbuf(name, [P, scales.shape[2]], U8)
+            for q in range(4):
+                queue.dma_start(
+                    tile[32 * q : 32 * q + 32, :].bitcast(I32),
+                    scales[0, 4 * q : 4 * q + 4, :].bitcast(I32).partition_broadcast(8),
+                )
+            return tile
+
+        def load_rows(name, rows, queue=nc.sync):
+            tile = sbuf(name, [P, PACK, rows.shape[1]], F32)
+            queue.dma_start(tile[:], rows.rearrange("(p j) c -> p j c", j=PACK))
+            return tile
+
+        w1_raw = load_rows("w1_raw", w1)
+        xs_tab = load_scales("xs_tab", x_scales, nc.sync)
+        offs_t = load_list("offs_t", offs)
+        xw_tab = load_words("xw_tab", x_words, nc.sync)
+        unit_t = sbuf("unit_t", [P, PACK], F32)
+        nc.sync.dma_start(unit_t[:], unit.rearrange("(p j) o -> p (j o)", j=PACK))
+        c2_t = load_list("c2_t", c2)
+        ew_tab = load_words("ew_tab", e_words, nc.sync)
+        lv2_t = load_list("lv2_t", lv2)
+        w2_raw = load_rows("w2_raw", w2)
+        es_tab = load_scales("es_tab", e_scales, nc.sync)
+        c1_t = load_list("c1_t", c1)
+        gn_rows = gn.rearrange("(p j) c -> p j c", j=PACK)
+        gn_t = {}
+        for h in range(2):
+            for jj in range(2):
+                tile = sbuf("gn_%d_%d" % (h, jj), [P, 2, HALF], F32)
+                nc.sync.dma_start(tile[:], gn_rows[:, 2 * jj : 2 * jj + 2, h * HALF : (h + 1) * HALF])
+                gn_t[h, 2 * jj] = tile[:, 0, :]
+                gn_t[h, 2 * jj + 1] = tile[:, 1, :]
+            if h == 0:
+                w3_raw = load_rows("w3_raw", w3)
+        feat_t = sbuf("feat_t", [P, 2, U], F32)
+        nc.sync.dma_start(feat_t[:], feat.rearrange("(a p) r -> p a r", p=P))
+
+        zeros = sbuf("zeros", [P, SPARE], F32)
+        nc.vector.memset(zeros[:], 0.0)
+        y_win = [sbuf("y_%d" % t, [P, S + SPARE], F32) for t in range(PACK)]
+        ye_win = [sbuf("ye_%d" % t, [P, S + SPARE], F32) for t in range(PACK)]
+        for win in y_win + ye_win:
+            nc.scalar.copy(win[:, S:], zeros[:])
+
+        sign = sbuf("sign", [P, PACK], F32)
+        size = sbuf("size", [P, PACK], F32)
+        nonneg = sbuf("nonneg", [P, PACK], F32)
+        nc.vector.tensor_scalar(nonneg[:], unit_t[:], 0.0, 2.0, ALU.is_ge, ALU.mult)
+        nc.vector.tensor_scalar(sign[:], nonneg[:], 1.0, -1.0, ALU.mult, ALU.add)
+        nc.vector.tensor_tensor(size[:], unit_t[:], sign[:], ALU.mult)
+
+        def deal(eng_copy, grouped, raw, m0, m1):
+            eng_copy(
+                grouped[:].rearrange("p (t m j) -> p m j t", t=PACK, j=PACK)[:, m0:m1],
+                raw[:].rearrange("p j (m t) -> p m j t", t=PACK)[:, m0:m1],
+            )
+
+        def quantise(name, grouped, cols):
+            codes = sbuf(name + "_codes", [P, cols], U32)
+            scales = sbuf(name + "_scales", [P, cols], U8)
+            nc.vector.quantize_mx(out=codes[:].bitcast(FP8X4), scales=scales[:], in_=grouped)
+            return codes, scales
+
+        def pick(name, words, scales, lst):
+            pw = sbuf(name + "_pw", [P, S], U32)
+            ps = sbuf(name + "_ps", [P, S], U8)
+            nc.vector.tensor_copy(ps[:], scales[:].indirect(lst[:]))
+            nc.vector.tensor_copy(pw[:], words[:].indirect(lst[:]))
+            return pw, ps
+
+        def project(wq, picked, wins):
+            for t in range(PACK):
+                acc = psum.tile([P, S], F32, name="acc")
+                nc.tensor.matmul_mx(
+                    out=acc[:],
+                    lhsT=wq[0][:, t * P : (t + 1) * P].bitcast(FP8X4),
+                    lhsT_scale=wq[1][:, t * P : (t + 1) * P],
+                    rhs=picked[0][:].bitcast(FP8X4),
+                    rhs_scale=picked[1][:],
+                    start=True,
+                    stop=True,
+                )
+                nc.scalar.activation(wins[t][:, :S], acc[:], COPY, scale=size[:, t : t + 1])
+
+        w1_g = sbuf("w1_g", [P, PACK * H], BF16)
+        deal(nc.vector.tensor_copy, w1_g, w1_raw, 0, 64)
+        deal(nc.scalar.copy, w1_g, w1_raw, 64, 128)
+        w1_q = quantise("w1", w1_g[:], H)
+        x_pick = pick("x", xw_tab, xs_tab, offs_t)
+        project(w1_q, x_pick, y_win)
+        e_pick = pick("e", ew_tab, es_tab, lv2_t)
+
+        w2_g = sbuf("w2_g", [P, PACK * H], BF16)
+        deal(nc.scalar.copy, w2_g, w2_raw, 0, 128)
+
+        def columns(lst, r0, n):
+            return lst[:, r0 // LIST : (r0 + n) // LIST]
+
+        floor = [sbuf("floor_%d" % h, [P, PACK, HALF], F32) for h in range(2)]
+        gained = [sbuf("gained_%d" % h, [P, PACK, HALF], F32) for h in range(2)]
+
+        def gather_floor(h):
+            for t in range(PACK):
+                nc.vector.tensor_copy(floor[h][:, t, :], y_win[t][:].indirect(columns(c2_t, h * HALF, HALF)))
+
+        def gather_gained(h):
+            for t in range(PACK):
+                nc.vector.tensor_tensor(
+                    gained[h][:, t, :], ye_win[t][:].indirect(columns(c2_t, h * HALF, HALF)), gn_t[h, t], ALU.mult
+                )
+
+        def weave(dst, n):
+            return dst[:].rearrange("p (c i t) -> p c t i", i=4, t=PACK)
+
+        def planes(src):
+            return src.rearrange("p t (c i) -> p c t i", i=4)
+
+        floor_w = [sbuf("floor_w_%d" % h, [P, PACK * HALF], BF16) for h in range(2)]
+
+        def weave_floor(h):
+            nc.scalar.activation(weave(floor_w[h], HALF), planes(floor[h][:]), COPY, scale=0.7)
+
+        gather_floor(0)
+        w2_q = quantise("w2", w2_g[:], H)
+        project(w2_q, e_pick, ye_win)
+        weave_floor(0)
+        gather_floor(1)
+
+        w3_s = sbuf("w3_s", [P, PACK, N], BF16)
+        for j in range(PACK):
+            nc.scalar.activation(w3_s[:, j, :], w3_raw[:, j, :], COPY, scale=sign[:, j : j + 1])
+        w3_g = sbuf("w3_g", [P, PACK * N], BF16)
+        nc.scalar.copy(weave(w3_g, N), planes(w3_s[:]))
+        weave_floor(1)
+
+        rec_w = {}
+
+        def gather_rec(c):
+            r0, n = CHUNKS[c]
+            h, o = divmod(r0, HALF)
+            rec = sbuf("rec_%d" % c, [P, PACK, n], F32)
+            for t in range(PACK):
+                nc.vector.tensor_tensor(
+                    rec[:, t, :], y_win[t][:].indirect(columns(c1_t, r0, n)), gained[h][:, t, o : o + n], ALU.add
+                )
+            rec_w[c] = sbuf("rec_w_%d" % c, [P, PACK * n], BF16)
+            nc.scalar.copy(weave(rec_w[c], n), planes(rec[:]))
+
+        hid = {}
+        hid_q = {}
+        accs = {}
+
+        def top(c):
+            r0, n = CHUNKS[c]
+            h, o = divmod(r0, HALF)
+            hid[c] = sbuf("hid_%d" % c, [P, PACK * n], BF16)
+            nc.vector.tensor_tensor(hid[c][:], rec_w[c][:], floor_w[h][:, PACK * o : PACK * (o + n)], ALU.max)
+
+        def product(c):
+            r0, n = CHUNKS[c]
+            hid_q[c] = quantise("hid_%d" % c, hid[c][:], n)
+            accs[c] = []
+            for a in range(2):
+                acc = psum.tile([P, S], F32, name="acc")
+                nc.tensor.matmul_mx(
+                    out=acc[:, :n],
+                    lhsT=w3_q[0][:, a * P : (a + 1) * P].bitcast(FP8X4),
+                    lhsT_scale=w3_q[1][:, a * P : (a + 1) * P],
+                    rhs=hid_q[c][0][:].bitcast(FP8X4),
+                    rhs_scale=hid_q[c][1][:],
+                    start=True,
+                    stop=True,
+                )
+                accs[c].append(acc)
+
+        def finish(c):
+            r0, n = CHUNKS[c]
+            for a in range(2):
+                res = sbuf("res_%d_%d" % (c, a), [P, n], F32)
+                nc.vector.tensor_tensor(res[:], accs[c][a][:, :n], feat_t[:, a, r0 : r0 + n], ALU.mult)
+                nc.sync.dma_start(out[a * P : (a + 1) * P, r0 : r0 + n], res[:])
+
+        gather_gained(0)
+        gather_rec(0)
+        w3_q = quantise("w3", w3_g[:], N)
+        gather_gained(1)
+        top(0)
+        gather_rec(1)
+        product(0)
+        gather_rec(2)
+        top(1)
+        finish(0)
+        product(1)
+        top(2)
+        finish(1)
+        product(2)
+        finish(2)

@@ -31,8 +31,8 @@ def tile_picked_ysemid_max_p_kernel(
         keep = ctx.enter_context(tc.tile_pool(name="keep", bufs=1))
         psum = ctx.enter_context(tc.psum_pool(name="psum", bufs=8))
 
-        def sbuf(name, shape, dtype):
-            return keep.tile(shape, dtype, name=name, align_bytes=64)
+        def sbuf(name, shape, dtype, slot=None):
+            return keep.tile(shape, dtype, name=name, tag=slot or name, align_bytes=64)
 
         def load_list(name, src):
             tile = keep.tile(list(src.shape), U16, name=name)
@@ -58,28 +58,32 @@ def tile_picked_ysemid_max_p_kernel(
             queue.dma_start(tile[:], rows.rearrange("(p j) c -> p j c", j=PACK))
             return tile
 
-        w1_raw = load_rows("w1_raw", w1)
-        xs_tab = load_scales("xs_tab", x_scales, nc.sync)
-        offs_t = load_list("offs_t", offs)
-        xw_tab = load_words("xw_tab", x_words, nc.sync)
+        gn_rows = gn.rearrange("(p j) c -> p j c", j=PACK)
+        gn_t = {}
+
+        def load_gains(h, jj):
+            tile = sbuf("gn_%d_%d" % (h, jj), [P, 2, HALF], F32)
+            nc.sync.dma_start(tile[:], gn_rows[:, 2 * jj : 2 * jj + 2, h * HALF : (h + 1) * HALF])
+            gn_t[h, 2 * jj] = tile[:, 0, :]
+            gn_t[h, 2 * jj + 1] = tile[:, 1, :]
+
+        es_tab = load_scales("es_tab", e_scales, nc.sync)
+        lv2_t = load_list("lv2_t", lv2)
+        w2_raw = load_rows("w2_raw", w2)
+        ew_tab = load_words("ew_tab", e_words, nc.sync)
         unit_t = sbuf("unit_t", [P, PACK], F32)
         nc.sync.dma_start(unit_t[:], unit.rearrange("(p j) o -> p (j o)", j=PACK))
         c2_t = load_list("c2_t", c2)
-        ew_tab = load_words("ew_tab", e_words, nc.sync)
-        lv2_t = load_list("lv2_t", lv2)
-        w2_raw = load_rows("w2_raw", w2)
-        es_tab = load_scales("es_tab", e_scales, nc.sync)
+        xs_tab = load_scales("xs_tab", x_scales, nc.sync)
+        load_gains(0, 0)
+        offs_t = load_list("offs_t", offs)
+        load_gains(0, 1)
+        xw_tab = load_words("xw_tab", x_words, nc.sync)
+        w1_raw = load_rows("w1_raw", w1)
+        load_gains(1, 0)
+        load_gains(1, 1)
         c1_t = load_list("c1_t", c1)
-        gn_rows = gn.rearrange("(p j) c -> p j c", j=PACK)
-        gn_t = {}
-        for h in range(2):
-            for jj in range(2):
-                tile = sbuf("gn_%d_%d" % (h, jj), [P, 2, HALF], F32)
-                nc.sync.dma_start(tile[:], gn_rows[:, 2 * jj : 2 * jj + 2, h * HALF : (h + 1) * HALF])
-                gn_t[h, 2 * jj] = tile[:, 0, :]
-                gn_t[h, 2 * jj + 1] = tile[:, 1, :]
-            if h == 0:
-                w3_raw = load_rows("w3_raw", w3)
+        w3_raw = load_rows("w3_raw", w3)
         feat_t = sbuf("feat_t", [P, 2, U], F32)
         nc.sync.dma_start(feat_t[:], feat.rearrange("(a p) r -> p a r", p=P))
 
@@ -109,6 +113,15 @@ def tile_picked_ysemid_max_p_kernel(
             nc.vector.quantize_mx(out=codes[:].bitcast(FP8X4), scales=scales[:], in_=grouped)
             return codes, scales
 
+        def quantise_dealt(name, grouped):
+            pieces = {}
+            for t0, t1 in ((0, 1), (1, 2), (2, 4)):
+                codes, scales = quantise("%s_%d" % (name, t0), grouped[:, t0 * H : t1 * H], (t1 - t0) * P)
+                for t in range(t0, t1):
+                    cols = slice((t - t0) * P, (t - t0 + 1) * P)
+                    pieces[t] = (codes[:, cols], scales[:, cols])
+            return pieces
+
         def pick(name, words, scales, lst):
             pw = sbuf(name + "_pw", [P, S], U32)
             ps = sbuf(name + "_ps", [P, S], U8)
@@ -121,8 +134,8 @@ def tile_picked_ysemid_max_p_kernel(
                 acc = psum.tile([P, S], F32, name="acc")
                 nc.tensor.matmul_mx(
                     out=acc[:],
-                    lhsT=wq[0][:, t * P : (t + 1) * P].bitcast(FP8X4),
-                    lhsT_scale=wq[1][:, t * P : (t + 1) * P],
+                    lhsT=wq[t][0].bitcast(FP8X4),
+                    lhsT_scale=wq[t][1],
                     rhs=picked[0][:].bitcast(FP8X4),
                     rhs_scale=picked[1][:],
                     start=True,
@@ -130,31 +143,24 @@ def tile_picked_ysemid_max_p_kernel(
                 )
                 nc.scalar.activation(wins[t][:, :S], acc[:], COPY, scale=size[:, t : t + 1])
 
-        w1_g = sbuf("w1_g", [P, PACK * H], BF16)
-        deal(nc.vector.tensor_copy, w1_g, w1_raw, 0, 64)
-        deal(nc.scalar.copy, w1_g, w1_raw, 64, 128)
-        w1_q = quantise("w1", w1_g[:], H)
-        x_pick = pick("x", xw_tab, xs_tab, offs_t)
-        project(w1_q, x_pick, y_win)
-        e_pick = pick("e", ew_tab, es_tab, lv2_t)
-
-        w2_g = sbuf("w2_g", [P, PACK * H], BF16)
-        deal(nc.scalar.copy, w2_g, w2_raw, 0, 128)
-
         def columns(lst, r0, n):
             return lst[:, r0 // LIST : (r0 + n) // LIST]
 
-        floor = [sbuf("floor_%d" % h, [P, PACK, HALF], F32) for h in range(2)]
-        gained = [sbuf("gained_%d" % h, [P, PACK, HALF], F32) for h in range(2)]
+        floor = {}
+        gained = {}
+        floor_w = {}
 
-        def gather_floor(h):
+        def gather_floor(h, slot=None):
+            floor[h] = sbuf("floor_%d" % h, [P, PACK, HALF], F32, slot)
             for t in range(PACK):
                 nc.vector.tensor_copy(floor[h][:, t, :], y_win[t][:].indirect(columns(c2_t, h * HALF, HALF)))
 
-        def gather_gained(h):
-            for t in range(PACK):
+        def gather_gained(h, jj, slot=None):
+            tile = sbuf("gained_%d_%d" % (h, jj), [P, 2, HALF], F32, slot)
+            for t in range(2 * jj, 2 * jj + 2):
+                gained[h, t] = tile[:, t % 2, :]
                 nc.vector.tensor_tensor(
-                    gained[h][:, t, :], ye_win[t][:].indirect(columns(c2_t, h * HALF, HALF)), gn_t[h, t], ALU.mult
+                    gained[h, t], ye_win[t][:].indirect(columns(c2_t, h * HALF, HALF)), gn_t[h, t], ALU.mult
                 )
 
         def weave(dst, n):
@@ -163,33 +169,19 @@ def tile_picked_ysemid_max_p_kernel(
         def planes(src):
             return src.rearrange("p t (c i) -> p c t i", i=4)
 
-        floor_w = [sbuf("floor_w_%d" % h, [P, PACK * HALF], BF16) for h in range(2)]
-
-        def weave_floor(h):
+        def weave_floor(h, slot=None):
+            floor_w[h] = sbuf("floor_w_%d" % h, [P, PACK * HALF], BF16, slot)
             nc.scalar.activation(weave(floor_w[h], HALF), planes(floor[h][:]), COPY, scale=0.7)
-
-        gather_floor(0)
-        w2_q = quantise("w2", w2_g[:], H)
-        project(w2_q, e_pick, ye_win)
-        weave_floor(0)
-        gather_floor(1)
-
-        w3_s = sbuf("w3_s", [P, PACK, N], BF16)
-        for j in range(PACK):
-            nc.scalar.activation(w3_s[:, j, :], w3_raw[:, j, :], COPY, scale=sign[:, j : j + 1])
-        w3_g = sbuf("w3_g", [P, PACK * N], BF16)
-        nc.scalar.copy(weave(w3_g, N), planes(w3_s[:]))
-        weave_floor(1)
 
         rec_w = {}
 
-        def gather_rec(c):
+        def gather_rec(c, slot=None):
             r0, n = CHUNKS[c]
             h, o = divmod(r0, HALF)
-            rec = sbuf("rec_%d" % c, [P, PACK, n], F32)
+            rec = sbuf("rec_%d" % c, [P, PACK, n], F32, slot)
             for t in range(PACK):
                 nc.vector.tensor_tensor(
-                    rec[:, t, :], y_win[t][:].indirect(columns(c1_t, r0, n)), gained[h][:, t, o : o + n], ALU.add
+                    rec[:, t, :], y_win[t][:].indirect(columns(c1_t, r0, n)), gained[h, t][:, o : o + n], ALU.add
                 )
             rec_w[c] = sbuf("rec_w_%d" % c, [P, PACK * n], BF16)
             nc.scalar.copy(weave(rec_w[c], n), planes(rec[:]))
@@ -204,14 +196,13 @@ def tile_picked_ysemid_max_p_kernel(
             hid[c] = sbuf("hid_%d" % c, [P, PACK * n], BF16)
             nc.vector.tensor_tensor(hid[c][:], rec_w[c][:], floor_w[h][:, PACK * o : PACK * (o + n)], ALU.max)
 
-        def product(c):
+        def product(c, banks):
             r0, n = CHUNKS[c]
             hid_q[c] = quantise("hid_%d" % c, hid[c][:], n)
-            accs[c] = []
+            accs[c] = [psum.tile([P, 2 // banks, n], F32, name="acc") for b in range(banks)]
             for a in range(2):
-                acc = psum.tile([P, S], F32, name="acc")
                 nc.tensor.matmul_mx(
-                    out=acc[:, :n],
+                    out=accs[c][a * banks // 2][:, a % (2 // banks), :],
                     lhsT=w3_q[0][:, a * P : (a + 1) * P].bitcast(FP8X4),
                     lhsT_scale=w3_q[1][:, a * P : (a + 1) * P],
                     rhs=hid_q[c][0][:].bitcast(FP8X4),
@@ -219,27 +210,54 @@ def tile_picked_ysemid_max_p_kernel(
                     start=True,
                     stop=True,
                 )
-                accs[c].append(acc)
+
+        out_rows = out.rearrange("(a p) r -> p a r", p=P)
 
         def finish(c):
             r0, n = CHUNKS[c]
-            for a in range(2):
-                res = sbuf("res_%d_%d" % (c, a), [P, n], F32)
-                nc.vector.tensor_tensor(res[:], accs[c][a][:, :n], feat_t[:, a, r0 : r0 + n], ALU.mult)
-                nc.sync.dma_start(out[a * P : (a + 1) * P, r0 : r0 + n], res[:])
+            per = 2 // len(accs[c])
+            for b, acc in enumerate(accs[c]):
+                res = sbuf("res_%d_%d" % (c, b), [P, per, n], F32)
+                rows = slice(b * per, (b + 1) * per)
+                nc.vector.tensor_tensor(res[:], acc[:], feat_t[:, rows, r0 : r0 + n], ALU.mult)
+                nc.sync.dma_start(out_rows[:, rows, r0 : r0 + n], res[:])
 
-        gather_gained(0)
+        w2_g = sbuf("w2_g", [P, PACK * H], BF16)
+        deal(nc.vector.tensor_copy, w2_g, w2_raw, 0, 64)
+        deal(nc.scalar.copy, w2_g, w2_raw, 64, 128)
+        w2_q = quantise_dealt("w2", w2_g)
+        e_pick = pick("e", ew_tab, es_tab, lv2_t)
+        project(w2_q, e_pick, ye_win)
+        gather_gained(0, 0)
+        gather_gained(0, 1)
+        x_pick = pick("x", xw_tab, xs_tab, offs_t)
+        w1_g = sbuf("w1_g", [P, PACK * H], BF16)
+        deal(nc.scalar.copy, w1_g, w1_raw, 0, 128)
+        gather_gained(1, 0)
+        w1_q = quantise("w1", w1_g[:], H)
+        project([(w1_q[0][:, t * P : (t + 1) * P], w1_q[1][:, t * P : (t + 1) * P]) for t in range(PACK)], x_pick, y_win)
+        gather_gained(1, 1, "w1_g")
+
+        w3_s = sbuf("w3_s", [P, PACK, N], BF16)
+        for j in range(PACK):
+            nc.scalar.activation(w3_s[:, j, :], w3_raw[:, j, :], COPY, scale=sign[:, j : j + 1])
+        w3_g = sbuf("w3_g", [P, PACK * N], BF16)
+        nc.scalar.copy(weave(w3_g, N), planes(w3_s[:]))
+
         gather_rec(0)
+        gather_floor(0)
+        weave_floor(0)
         w3_q = quantise("w3", w3_g[:], N)
-        gather_gained(1)
+        gather_floor(1, "gained_0_1")
+        weave_floor(1)
         top(0)
-        gather_rec(1)
-        product(0)
-        gather_rec(2)
-        top(1)
+        gather_rec(1, "rec_w_0")
+        product(0, 2)
+        gather_rec(2, "hid_0")
         finish(0)
-        product(1)
+        top(1)
+        product(1, 1)
         top(2)
         finish(1)
-        product(2)
+        product(2, 2)
         finish(2)

@@ -14,6 +14,7 @@ U8 = mybir.dt.uint8
 FP8X4 = mybir.dt.float8_e4m3fn_x4
 ALU = mybir.AluOpType
 COPY = mybir.ActivationFunctionType.Copy
+ABS = mybir.ActivationFunctionType.Abs
 
 P = 128
 PACK = 4
@@ -59,29 +60,30 @@ def tile_picked_ysemid_max_p_kernel(
             return tile
 
         gn_rows = gn.rearrange("(p j) c -> p j c", j=PACK)
-        gn_t = {}
 
-        def load_gains(h, jj):
-            tile = sbuf("gn_%d_%d" % (h, jj), [P, 2, HALF], F32)
-            nc.sync.dma_start(tile[:], gn_rows[:, 2 * jj : 2 * jj + 2, h * HALF : (h + 1) * HALF])
-            gn_t[h, 2 * jj] = tile[:, 0, :]
-            gn_t[h, 2 * jj + 1] = tile[:, 1, :]
+        def load_gains(t):
+            tile = sbuf("gn_%d" % t, [P, U], F32)
+            nc.sync.dma_start(tile[:], gn_rows[:, t, :])
+            return tile
+
+        def load_halves(name, w):
+            return [load_rows("%s_%d" % (name, h), w[:, h * H // 2 : (h + 1) * H // 2]) for h in range(2)]
 
         es_tab = load_scales("es_tab", e_scales, nc.sync)
         lv2_t = load_list("lv2_t", lv2)
-        w2_raw = load_rows("w2_raw", w2)
         ew_tab = load_words("ew_tab", e_words, nc.sync)
+        w2_raw = load_halves("w2_raw", w2)
+        xs_tab = load_scales("xs_tab", x_scales, nc.sync)
         unit_t = sbuf("unit_t", [P, PACK], F32)
         nc.sync.dma_start(unit_t[:], unit.rearrange("(p j) o -> p (j o)", j=PACK))
-        c2_t = load_list("c2_t", c2)
-        xs_tab = load_scales("xs_tab", x_scales, nc.sync)
-        load_gains(0, 0)
         offs_t = load_list("offs_t", offs)
-        load_gains(0, 1)
+        gn_t = [load_gains(0)]
+        c2_t = load_list("c2_t", c2)
+        gn_t.append(load_gains(1))
         xw_tab = load_words("xw_tab", x_words, nc.sync)
-        w1_raw = load_rows("w1_raw", w1)
-        load_gains(1, 0)
-        load_gains(1, 1)
+        gn_t.append(load_gains(2))
+        w1_raw = load_halves("w1_raw", w1)
+        gn_t.append(load_gains(3))
         c1_t = load_list("c1_t", c1)
         w3_raw = load_rows("w3_raw", w3)
         feat_t = sbuf("feat_t", [P, 2, U], F32)
@@ -90,21 +92,22 @@ def tile_picked_ysemid_max_p_kernel(
         zeros = sbuf("zeros", [P, SPARE], F32)
         nc.vector.memset(zeros[:], 0.0)
         y_win = [sbuf("y_%d" % t, [P, S + SPARE], F32) for t in range(PACK)]
-        ye_win = [sbuf("ye_%d" % t, [P, S + SPARE], F32) for t in range(PACK)]
-        for win in y_win + ye_win:
-            nc.scalar.copy(win[:, S:], zeros[:])
+        ye_win = [sbuf("ye_%d" % t, [P, U + SPARE], F32) for t in range(PACK)]
+        for t in range(PACK):
+            nc.scalar.copy(y_win[t][:, S:], zeros[:])
+            nc.gpsimd.memset(ye_win[t][:, S:], 0.0)
 
         sign = sbuf("sign", [P, PACK], F32)
         size = sbuf("size", [P, PACK], F32)
         nonneg = sbuf("nonneg", [P, PACK], F32)
-        nc.vector.tensor_scalar(nonneg[:], unit_t[:], 0.0, 2.0, ALU.is_ge, ALU.mult)
-        nc.vector.tensor_scalar(sign[:], nonneg[:], 1.0, -1.0, ALU.mult, ALU.add)
-        nc.vector.tensor_tensor(size[:], unit_t[:], sign[:], ALU.mult)
+        nc.scalar.activation(size[:], unit_t[:], ABS)
+        nc.gpsimd.tensor_scalar(nonneg[:], unit_t[:], 0.0, 2.0, ALU.is_ge, ALU.mult)
+        nc.gpsimd.tensor_scalar(sign[:], nonneg[:], 1.0, -1.0, ALU.mult, ALU.add)
 
-        def deal(eng_copy, grouped, raw, m0, m1):
+        def deal(eng_copy, grouped, raw, h, m0, m1):
             eng_copy(
-                grouped[:].rearrange("p (t m j) -> p m j t", t=PACK, j=PACK)[:, m0:m1],
-                raw[:].rearrange("p j (m t) -> p m j t", t=PACK)[:, m0:m1],
+                grouped[:].rearrange("p (t m j) -> p m j t", t=PACK, j=PACK)[:, 64 * h + m0 : 64 * h + m1],
+                raw[h][:].rearrange("p j (m t) -> p m j t", t=PACK)[:, m0:m1],
             )
 
         def quantise(name, grouped, cols):
@@ -155,13 +158,9 @@ def tile_picked_ysemid_max_p_kernel(
             for t in range(PACK):
                 nc.vector.tensor_copy(floor[h][:, t, :], y_win[t][:].indirect(columns(c2_t, h * HALF, HALF)))
 
-        def gather_gained(h, jj, slot=None):
-            tile = sbuf("gained_%d_%d" % (h, jj), [P, 2, HALF], F32, slot)
-            for t in range(2 * jj, 2 * jj + 2):
-                gained[h, t] = tile[:, t % 2, :]
-                nc.vector.tensor_tensor(
-                    gained[h, t], ye_win[t][:].indirect(columns(c2_t, h * HALF, HALF)), gn_t[h, t], ALU.mult
-                )
+        def gather_gained(t, slot=None):
+            gained[t] = sbuf("gained_%d" % t, [P, U], F32, slot)
+            nc.vector.tensor_tensor(gained[t][:], ye_win[t][:].indirect(c2_t[:]), gn_t[t][:], ALU.mult)
 
         def weave(dst, n):
             return dst[:].rearrange("p (c i t) -> p c t i", i=4, t=PACK)
@@ -177,11 +176,10 @@ def tile_picked_ysemid_max_p_kernel(
 
         def gather_rec(c, slot=None):
             r0, n = CHUNKS[c]
-            h, o = divmod(r0, HALF)
             rec = sbuf("rec_%d" % c, [P, PACK, n], F32, slot)
             for t in range(PACK):
                 nc.vector.tensor_tensor(
-                    rec[:, t, :], y_win[t][:].indirect(columns(c1_t, r0, n)), gained[h, t][:, o : o + n], ALU.add
+                    rec[:, t, :], y_win[t][:].indirect(columns(c1_t, r0, n)), gained[t][:, r0 : r0 + n], ALU.add
                 )
             rec_w[c] = sbuf("rec_w_%d" % c, [P, PACK * n], BF16)
             nc.scalar.copy(weave(rec_w[c], n), planes(rec[:]))
@@ -223,20 +221,22 @@ def tile_picked_ysemid_max_p_kernel(
                 nc.sync.dma_start(out_rows[:, rows, r0 : r0 + n], res[:])
 
         w2_g = sbuf("w2_g", [P, PACK * H], BF16)
-        deal(nc.vector.tensor_copy, w2_g, w2_raw, 0, 64)
-        deal(nc.scalar.copy, w2_g, w2_raw, 64, 128)
-        w2_q = quantise_dealt("w2", w2_g)
+        deal(nc.scalar.copy, w2_g, w2_raw, 0, 0, 64)
+        deal(nc.scalar.copy, w2_g, w2_raw, 1, 0, 32)
         e_pick = pick("e", ew_tab, es_tab, lv2_t)
+        deal(nc.vector.tensor_copy, w2_g, w2_raw, 1, 32, 64)
+        w2_q = quantise_dealt("w2", w2_g)
         project(w2_q, e_pick, ye_win)
-        gather_gained(0, 0)
-        gather_gained(0, 1)
+        gather_gained(0)
+        gather_gained(1)
         x_pick = pick("x", xw_tab, xs_tab, offs_t)
         w1_g = sbuf("w1_g", [P, PACK * H], BF16)
-        deal(nc.scalar.copy, w1_g, w1_raw, 0, 128)
-        gather_gained(1, 0)
+        deal(nc.scalar.copy, w1_g, w1_raw, 0, 0, 64)
+        deal(nc.scalar.copy, w1_g, w1_raw, 1, 0, 64)
+        gather_gained(2)
         w1_q = quantise("w1", w1_g[:], H)
         project([(w1_q[0][:, t * P : (t + 1) * P], w1_q[1][:, t * P : (t + 1) * P]) for t in range(PACK)], x_pick, y_win)
-        gather_gained(1, 1, "w1_g")
+        gather_gained(3, "w1_g")
 
         w3_s = sbuf("w3_s", [P, PACK, N], BF16)
         for j in range(PACK):
@@ -248,7 +248,7 @@ def tile_picked_ysemid_max_p_kernel(
         gather_floor(0)
         weave_floor(0)
         w3_q = quantise("w3", w3_g[:], N)
-        gather_floor(1, "gained_0_1")
+        gather_floor(1, "size")
         weave_floor(1)
         top(0)
         gather_rec(1, "rec_w_0")

@@ -153,10 +153,12 @@ def tile_picked_ysemid_max_p_kernel(
         gained = {}
         floor_w = {}
 
-        def gather_floor(h, slot=None):
-            floor[h] = sbuf("floor_%d" % h, [P, PACK, HALF], F32, slot)
-            for t in range(PACK):
-                nc.vector.tensor_copy(floor[h][:, t, :], y_win[t][:].indirect(columns(c2_t, h * HALF, HALF)))
+        def gather_floor(c, tiles, slot=None):
+            r0, n = CHUNKS[c]
+            if c not in floor:
+                floor[c] = sbuf("floor_%d" % c, [P, PACK, n], F32, slot)
+            for t in tiles:
+                nc.vector.tensor_copy(floor[c][:, t, :], y_win[t][:].indirect(columns(c2_t, r0, n)))
 
         def gather_gained(t, slot=None):
             gained[t] = sbuf("gained_%d" % t, [P, U], F32, slot)
@@ -168,21 +170,27 @@ def tile_picked_ysemid_max_p_kernel(
         def planes(src):
             return src.rearrange("p t (c i) -> p c t i", i=4)
 
-        def weave_floor(h, slot=None):
-            floor_w[h] = sbuf("floor_w_%d" % h, [P, PACK * HALF], BF16, slot)
-            nc.scalar.activation(weave(floor_w[h], HALF), planes(floor[h][:]), COPY, scale=0.7)
+        def weave_floor(c):
+            n = CHUNKS[c][1]
+            floor_w[c] = sbuf("floor_w_%d" % c, [P, PACK * n], BF16)
+            nc.scalar.activation(weave(floor_w[c], n), planes(floor[c][:]), COPY, scale=0.7)
 
         rec_w = {}
 
-        def gather_rec(c, slot=None):
-            r0, n = CHUNKS[c]
-            rec = sbuf("rec_%d" % c, [P, PACK, n], F32, slot)
+        def gather_rec(h, slot=None):
+            rec = sbuf("rec_%d" % h, [P, PACK, HALF], F32, slot)
             for t in range(PACK):
                 nc.vector.tensor_tensor(
-                    rec[:, t, :], y_win[t][:].indirect(columns(c1_t, r0, n)), gained[t][:, r0 : r0 + n], ALU.add
+                    rec[:, t, :],
+                    y_win[t][:].indirect(columns(c1_t, h * HALF, HALF)),
+                    gained[t][:, h * HALF : (h + 1) * HALF],
+                    ALU.add,
                 )
-            rec_w[c] = sbuf("rec_w_%d" % c, [P, PACK * n], BF16)
-            nc.scalar.copy(weave(rec_w[c], n), planes(rec[:]))
+            return rec
+
+        def weave_rec(h, rec):
+            rec_w[h] = sbuf("rec_w_%d" % h, [P, PACK * HALF], BF16)
+            nc.scalar.copy(weave(rec_w[h], HALF), planes(rec[:]))
 
         hid = {}
         hid_q = {}
@@ -192,7 +200,7 @@ def tile_picked_ysemid_max_p_kernel(
             r0, n = CHUNKS[c]
             h, o = divmod(r0, HALF)
             hid[c] = sbuf("hid_%d" % c, [P, PACK * n], BF16)
-            nc.vector.tensor_tensor(hid[c][:], rec_w[c][:], floor_w[h][:, PACK * o : PACK * (o + n)], ALU.max)
+            nc.vector.tensor_tensor(hid[c][:], rec_w[h][:, PACK * o : PACK * (o + n)], floor_w[c][:], ALU.max)
 
         def product(c, banks):
             r0, n = CHUNKS[c]
@@ -220,6 +228,15 @@ def tile_picked_ysemid_max_p_kernel(
                 nc.vector.tensor_tensor(res[:], acc[:], feat_t[:, rows, r0 : r0 + n], ALU.mult)
                 nc.sync.dma_start(out_rows[:, rows, r0 : r0 + n], res[:])
 
+        def finish_aside(c):
+            r0, n = CHUNKS[c]
+            for a, acc in enumerate(accs[c]):
+                sums = sbuf("sums_%d" % a, [P, n], F32)
+                nc.scalar.copy(sums[:], acc[:, 0, :])
+                res = sbuf("res_aside_%d" % a, [P, n], F32)
+                nc.gpsimd.tensor_tensor(res[:], sums[:], feat_t[:, a, r0 : r0 + n], ALU.mult)
+                nc.sync.dma_start(out_rows[:, a, r0 : r0 + n], res[:])
+
         w2_g = sbuf("w2_g", [P, PACK * H], BF16)
         deal(nc.scalar.copy, w2_g, w2_raw, 0, 0, 64)
         deal(nc.scalar.copy, w2_g, w2_raw, 1, 0, 32)
@@ -244,17 +261,19 @@ def tile_picked_ysemid_max_p_kernel(
         w3_g = sbuf("w3_g", [P, PACK * N], BF16)
         nc.scalar.copy(weave(w3_g, N), planes(w3_s[:]))
 
-        gather_rec(0)
-        gather_floor(0)
+        weave_rec(0, gather_rec(0))
+        gather_floor(0, range(PACK))
         weave_floor(0)
         w3_q = quantise("w3", w3_g[:], N)
-        gather_floor(1, "size")
-        weave_floor(1)
+        weave_rec(1, gather_rec(1, "size"))
         top(0)
-        gather_rec(1, "rec_w_0")
+        gather_floor(1, range(1), "rec_w_0")
         product(0, 2)
-        gather_rec(2, "hid_0")
-        finish(0)
+        finish_aside(0)
+        gather_floor(1, range(1, PACK))
+        weave_floor(1)
+        gather_floor(2, range(PACK), "floor_w_0")
+        weave_floor(2)
         top(1)
         product(1, 1)
         top(2)

from contextlib import ExitStack

import concourse.mybir as mybir

K, T, S, N, H, U, W = 512, 2048, 512, 256, 512, 1024, 1024
FLOPS = 2 * (2 * K * H * S + H * N * U)

F32 = mybir.dt.float32
BF16 = mybir.dt.bfloat16
I32 = mybir.dt.int32
U32 = mybir.dt.uint32
U16 = mybir.dt.uint16
U8 = mybir.dt.uint8
FP8X4 = mybir.dt.float8_e4m3fn_x4
ALU = mybir.AluOpType
COPY = mybir.ActivationFunctionType.Copy
ABS = mybir.ActivationFunctionType.Abs

P = 128
PACK = 4
LIST = 16
SPARE = 16
HALF = 512
CHUNKS = ((0, 512), (512, 256), (768, 256))


def tile_picked_ysemid_max_p_kernel(
    tc, x_words, x_scales, w1, e_words, e_scales, w2, gn, unit, w3, feat, offs, lv2, c1, c2, out
):
    nc = tc.nc
    with ExitStack() as ctx:
        keep = ctx.enter_context(tc.tile_pool(name="keep", bufs=1))
        psum = ctx.enter_context(tc.psum_pool(name="psum", bufs=8))

        def sbuf(name, shape, dtype, slot=None):
            return keep.tile(shape, dtype, name=name, tag=slot or name, align_bytes=64)

        def load_list(name, src):
            tile = keep.tile(list(src.shape), U16, name=name)
            nc.sync.dma_start(tile[:], src)
            return tile

        def load_words(name, words, queue):
            tile = sbuf(name, [P, words.shape[2]], U32)
            queue.dma_start(tile[:].bitcast(I32), words[0].rearrange("p n t -> p (n t)").bitcast(I32))
            return tile

        def load_scales(name, scales, queue):
            tile = sbuf(name, [P, scales.shape[2]], U8)
            for q in range(4):
                queue.dma_start(
                    tile[32 * q : 32 * q + 32, :].bitcast(I32),
                    scales[0, 4 * q : 4 * q + 4, :].bitcast(I32).partition_broadcast(8),
                )
            return tile

        def load_rows(name, rows, queue=nc.sync):
            tile = sbuf(name, [P, PACK, rows.shape[1]], F32)
            queue.dma_start(tile[:], rows.rearrange("(p j) c -> p j c", j=PACK))
            return tile

        gn_rows = gn.rearrange("(p j) c -> p j c", j=PACK)

        def load_gains(t):
            tile = sbuf("gn_%d" % t, [P, U], F32)
            nc.sync.dma_start(tile[:], gn_rows[:, t, :])
            return tile

        def load_halves(name, w):
            return [load_rows("%s_%d" % (name, h), w[:, h * H // 2 : (h + 1) * H // 2]) for h in range(2)]

        es_tab = load_scales("es_tab", e_scales, nc.sync)
        lv2_t = load_list("lv2_t", lv2)
        ew_tab = load_words("ew_tab", e_words, nc.sync)
        w2_raw = load_halves("w2_raw", w2)
        xs_tab = load_scales("xs_tab", x_scales, nc.sync)
        unit_t = sbuf("unit_t", [P, PACK], F32)
        nc.sync.dma_start(unit_t[:], unit.rearrange("(p j) o -> p (j o)", j=PACK))
        offs_t = load_list("offs_t", offs)
        gn_t = [load_gains(0)]
        c2_t = load_list("c2_t", c2)
        gn_t.append(load_gains(1))
        xw_tab = load_words("xw_tab", x_words, nc.sync)
        gn_t.append(load_gains(2))
        w1_raw = load_halves("w1_raw", w1)
        gn_t.append(load_gains(3))
        c1_t = load_list("c1_t", c1)
        w3_raw = load_rows("w3_raw", w3)
        feat_t = sbuf("feat_t", [P, 2, U], F32)
        nc.sync.dma_start(feat_t[:], feat.rearrange("(a p) r -> p a r", p=P))

        zeros = sbuf("zeros", [P, SPARE], F32)
        nc.vector.memset(zeros[:], 0.0)
        y_win = [sbuf("y_%d" % t, [P, S + SPARE], F32) for t in range(PACK)]
        ye_win = [sbuf("ye_%d" % t, [P, U + SPARE], F32) for t in range(PACK)]
        for t in range(PACK):
            nc.scalar.copy(y_win[t][:, S:], zeros[:])
            nc.gpsimd.memset(ye_win[t][:, S:], 0.0)

        sign = sbuf("sign", [P, PACK], F32)
        size = sbuf("size", [P, PACK], F32)
        nonneg = sbuf("nonneg", [P, PACK], F32)
        nc.scalar.activation(size[:], unit_t[:], ABS)
        nc.gpsimd.tensor_scalar(nonneg[:], unit_t[:], 0.0, 2.0, ALU.is_ge, ALU.mult)
        nc.gpsimd.tensor_scalar(sign[:], nonneg[:], 1.0, -1.0, ALU.mult, ALU.add)

        def deal(eng_copy, grouped, raw, h, m0, m1):
            eng_copy(
                grouped[:].rearrange("p (t m j) -> p m j t", t=PACK, j=PACK)[:, 64 * h + m0 : 64 * h + m1],
                raw[h][:].rearrange("p j (m t) -> p m j t", t=PACK)[:, m0:m1],
            )

        def quantise(name, grouped, cols):
            codes = sbuf(name + "_codes", [P, cols], U32)
            scales = sbuf(name + "_scales", [P, cols], U8)
            nc.vector.quantize_mx(out=codes[:].bitcast(FP8X4), scales=scales[:], in_=grouped)
            return codes, scales

        def quantise_dealt(name, grouped):
            pieces = {}
            for t0, t1 in ((0, 1), (1, 2), (2, 4)):
                codes, scales = quantise("%s_%d" % (name, t0), grouped[:, t0 * H : t1 * H], (t1 - t0) * P)
                for t in range(t0, t1):
                    cols = slice((t - t0) * P, (t - t0 + 1) * P)
                    pieces[t] = (codes[:, cols], scales[:, cols])
            return pieces

        def pick(name, words, scales, lst):
            pw = sbuf(name + "_pw", [P, S], U32)
            ps = sbuf(name + "_ps", [P, S], U8)
            nc.vector.tensor_copy(ps[:], scales[:].indirect(lst[:]))
            nc.vector.tensor_copy(pw[:], words[:].indirect(lst[:]))
            return pw, ps

        def project(wq, picked, wins):
            for t in range(PACK):
                acc = psum.tile([P, S], F32, name="acc")
                nc.tensor.matmul_mx(
                    out=acc[:],
                    lhsT=wq[t][0].bitcast(FP8X4),
                    lhsT_scale=wq[t][1],
                    rhs=picked[0][:].bitcast(FP8X4),
                    rhs_scale=picked[1][:],
                    start=True,
                    stop=True,
                )
                nc.scalar.activation(wins[t][:, :S], acc[:], COPY, scale=size[:, t : t + 1])

        def columns(lst, r0, n):
            return lst[:, r0 // LIST : (r0 + n) // LIST]

        floor = {}
        gained = {}
        floor_w = {}

        def gather_floor(c, tiles, slot=None):
            r0, n = CHUNKS[c]
            if c not in floor:
                floor[c] = sbuf("floor_%d" % c, [P, PACK, n], F32, slot)
            for t in tiles:
                nc.vector.tensor_copy(floor[c][:, t, :], y_win[t][:].indirect(columns(c2_t, r0, n)))

        def gather_gained(t, slot=None):
            gained[t] = sbuf("gained_%d" % t, [P, U], F32, slot)
            nc.vector.tensor_tensor(gained[t][:], ye_win[t][:].indirect(c2_t[:]), gn_t[t][:], ALU.mult)

        def weave(dst, n):
            return dst[:].rearrange("p (c i t) -> p c t i", i=4, t=PACK)

        def planes(src):
            return src.rearrange("p t (c i) -> p c t i", i=4)

        def weave_floor(c):
            n = CHUNKS[c][1]
            floor_w[c] = sbuf("floor_w_%d" % c, [P, PACK * n], BF16)
            nc.scalar.activation(weave(floor_w[c], n), planes(floor[c][:]), COPY, scale=0.7)

        rec_w = {}

        def gather_rec(h, slot=None):
            rec = sbuf("rec_%d" % h, [P, PACK, HALF], F32, slot)
            for t in range(PACK):
                nc.vector.tensor_tensor(
                    rec[:, t, :],
                    y_win[t][:].indirect(columns(c1_t, h * HALF, HALF)),
                    gained[t][:, h * HALF : (h + 1) * HALF],
                    ALU.add,
                )
            return rec

        def weave_rec(h, rec):
            rec_w[h] = sbuf("rec_w_%d" % h, [P, PACK * HALF], BF16)
            nc.scalar.copy(weave(rec_w[h], HALF), planes(rec[:]))

        hid = {}
        hid_q = {}
        accs = {}

        def top(c):
            r0, n = CHUNKS[c]
            h, o = divmod(r0, HALF)
            hid[c] = sbuf("hid_%d" % c, [P, PACK * n], BF16)
            nc.vector.tensor_tensor(hid[c][:], rec_w[h][:, PACK * o : PACK * (o + n)], floor_w[c][:], ALU.max)

        def product(c, banks):
            r0, n = CHUNKS[c]
            hid_q[c] = quantise("hid_%d" % c, hid[c][:], n)
            accs[c] = [psum.tile([P, 2 // banks, n], F32, name="acc") for b in range(banks)]
            for a in range(2):
                nc.tensor.matmul_mx(
                    out=accs[c][a * banks // 2][:, a % (2 // banks), :],
                    lhsT=w3_q[0][:, a * P : (a + 1) * P].bitcast(FP8X4),
                    lhsT_scale=w3_q[1][:, a * P : (a + 1) * P],
                    rhs=hid_q[c][0][:].bitcast(FP8X4),
                    rhs_scale=hid_q[c][1][:],
                    start=True,
                    stop=True,
                )

        out_rows = out.rearrange("(a p) r -> p a r", p=P)

        def finish(c):
            r0, n = CHUNKS[c]
            per = 2 // len(accs[c])
            for b, acc in enumerate(accs[c]):
                res = sbuf("res_%d_%d" % (c, b), [P, per, n], F32)
                rows = slice(b * per, (b + 1) * per)
                nc.vector.tensor_tensor(res[:], acc[:], feat_t[:, rows, r0 : r0 + n], ALU.mult)
                nc.sync.dma_start(out_rows[:, rows, r0 : r0 + n], res[:])

        def finish_aside(c):
            r0, n = CHUNKS[c]
            for a, acc in enumerate(accs[c]):
                sums = sbuf("sums_%d" % a, [P, n], F32)
                nc.scalar.copy(sums[:], acc[:, 0, :])
                res = sbuf("res_aside_%d" % a, [P, n], F32)
                nc.gpsimd.tensor_tensor(res[:], sums[:], feat_t[:, a, r0 : r0 + n], ALU.mult)
                nc.sync.dma_start(out_rows[:, a, r0 : r0 + n], res[:])

        w2_g = sbuf("w2_g", [P, PACK * H], BF16)
        deal(nc.scalar.copy, w2_g, w2_raw, 0, 0, 64)
        deal(nc.scalar.copy, w2_g, w2_raw, 1, 0, 32)
        e_pick = pick("e", ew_tab, es_tab, lv2_t)
        deal(nc.vector.tensor_copy, w2_g, w2_raw, 1, 32, 64)
        w2_q = quantise_dealt("w2", w2_g)
        project(w2_q, e_pick, ye_win)
        gather_gained(0)
        gather_gained(1)
        x_pick = pick("x", xw_tab, xs_tab, offs_t)
        w1_g = sbuf("w1_g", [P, PACK * H], BF16)
        deal(nc.scalar.copy, w1_g, w1_raw, 0, 0, 64)
        deal(nc.scalar.copy, w1_g, w1_raw, 1, 0, 64)
        gather_gained(2)
        w1_q = quantise("w1", w1_g[:], H)
        project([(w1_q[0][:, t * P : (t + 1) * P], w1_q[1][:, t * P : (t + 1) * P]) for t in range(PACK)], x_pick, y_win)
        gather_gained(3, "w1_g")

        w3_s = sbuf("w3_s", [P, PACK, N], BF16)
        for j in range(PACK):
            nc.scalar.activation(w3_s[:, j, :], w3_raw[:, j, :], COPY, scale=sign[:, j : j + 1])
        w3_g = sbuf("w3_g", [P, PACK * N], BF16)
        nc.scalar.copy(weave(w3_g, N), planes(w3_s[:]))

        weave_rec(0, gather_rec(0))
        gather_floor(0, range(PACK))
        weave_floor(0)
        w3_q = quantise("w3", w3_g[:], N)
        weave_rec(1, gather_rec(1, "size"))
        top(0)
        gather_floor(1, range(1), "rec_w_0")
        product(0, 2)
        finish_aside(0)
        gather_floor(1, range(1, PACK))
        weave_floor(1)
        gather_floor(2, range(PACK), "floor_w_0")
        weave_floor(2)
        top(1)
        product(1, 1)
        top(2)
        finish(1)
        product(2, 2)
        finish(2)
